import numpy as np
import ml_dtypes


def mxq(x, axis, fmt="e4m3"):
    dtype, down = {"e4m3": (ml_dtypes.float8_e4m3fn, 7), "e5m2": (ml_dtypes.float8_e5m2, 14)}[fmt]
    v = np.moveaxis(np.asarray(x, np.float32).astype(ml_dtypes.bfloat16).astype(np.float64), axis, -1)
    blocks = v.reshape(v.shape[:-1] + (-1, 32))
    amax = np.abs(blocks).max(-1, keepdims=True)
    byte = np.maximum(np.where(amax > 0, np.frexp(amax)[1] - 1 + 127, 0) - down, 1)
    scale = np.exp2(byte - 127.0)
    codes = (blocks / scale).astype(np.float32).astype(dtype).astype(np.float64)
    return np.moveaxis((codes * scale).reshape(v.shape), -1, axis)


WIDE = False


def mx_kscale(k):
    if not WIDE:
        return np.ones(k)
    levels = np.array([30, -30])
    if k % 512:
        return np.exp2(np.random.permutation(np.resize(levels, k // 32))).repeat(32)
    a = np.empty((k // 512, 16))
    for p in range(k // 512):
        a[p, :8] = np.random.permutation(np.resize(levels, 8))
        for g in range(8):
            far = levels[np.abs(levels - a[p, g]) >= 10]
            a[p, g + 8] = far[np.random.randint(len(far))]
    return np.exp2(a.ravel()).repeat(32)


def f64(x):
    return np.asarray(x).astype(np.float64)


def striped(idx):
    return np.tile(np.asarray(idx).reshape(-1, 16).T, (8, 1)).astype(np.uint16)


def unstriped(offs):
    return offs[:16].T.reshape(-1).astype(np.int64)


E2M1 = np.array([0.0, 0.5, 1.0, 1.5, 2.0, 3.0, 4.0, 6.0, -0.0, -0.5, -1.0, -1.5, -2.0, -3.0, -4.0, -6.0])


def pack_weight(w, fmt):
    k, n = w.shape
    w = f64(np.asarray(w, np.float32).astype(ml_dtypes.bfloat16)).reshape(k // 32, 32, n)
    amax = np.abs(w).max(1)
    if fmt in ("e4m3", "e5m2"):
        byte = np.frexp(amax)[1] - 1 + 127 - (7 if fmt == "e4m3" else 14)
    else:
        mant, ex = np.frexp(amax / 6.0)
        byte = np.where(mant > 0.5, ex, ex - 1) + 127
    byte = np.clip(np.where(amax > 0, byte, 1), 1, 254)
    scaled = (w * np.exp2(127.0 - byte)[:, None, :]).reshape(k, n).astype(np.float32)
    by_word = np.ascontiguousarray(scaled.reshape(k // 512, 128, 4, n).transpose(0, 1, 3, 2))
    if fmt in ("e4m3", "e5m2"):
        words = by_word.astype(ml_dtypes.float8_e4m3fn if fmt == "e4m3" else ml_dtypes.float8_e5m2).view(np.uint8)
    else:
        c = by_word.astype(ml_dtypes.float4_e2m1fn).view(np.uint8) & 0xF
        words = (c[..., 0::2] | (c[..., 1::2] << 4)).reshape(k // 512, 128, 2 * n)
    return np.ascontiguousarray(words), np.ascontiguousarray(byte.astype(np.uint8).reshape(k // 512, 16, n))


def unpack_weight(words, scales, fmt):
    g, _, n = scales.shape
    words = np.ascontiguousarray(words).reshape(g, 128, n, -1)
    if fmt in ("e4m3", "e5m2"):
        vals = words.view(ml_dtypes.float8_e4m3fn if fmt == "e4m3" else ml_dtypes.float8_e5m2).astype(np.float64)
    else:
        nib = np.empty((g, 128, n, 4), np.uint8)
        nib[..., 0::2] = words & 0xF
        nib[..., 1::2] = words >> 4
        vals = E2M1[nib]
    vals = vals * np.repeat(np.exp2(scales.astype(np.float64) - 127.0), 8, axis=1)[..., None]
    return vals.transpose(0, 1, 3, 2).reshape(g * 512, n)


def e4m3fn_bytes(y):
    return np.clip(np.asarray(y, np.float64), -448.0, 448.0).astype(np.float32).astype(ml_dtypes.float8_e4m3fn).view(np.uint8)


def e4m3fn_values(b):
    return np.asarray(b, np.uint8).view(ml_dtypes.float8_e4m3fn).astype(np.float64)


K, T, J, R, F, Z, V, O, N = 512, 1024, 256, 512, 512, 1024, 1024, 128, 256


def setup_inputs():
    n = np.random.standard_normal
    idx = np.random.permutation(T)[:J]
    idx2 = np.random.permutation(Z)[:J]
    idx3 = np.random.permutation(J)[:O]
    idx4 = np.random.permutation(V)[:O]
    idx5 = np.random.permutation(J)[:O]
    fk = mx_kscale(K)
    ff = mx_kscale(F)
    fr = mx_kscale(R)
    xtp = pack_weight(n((K, T)) / fk[:, None], "e5m2")
    xop = pack_weight(n((F, Z)) / ff[:, None], "e4m3")
    wp = pack_weight(n((K, R)) * 1 / np.sqrt(K) * fk[:, None], "e2m1")
    w2p = pack_weight(n((F, R)) * 1 / np.sqrt(F) * ff[:, None] * fr, "e2m1")
    wbp = pack_weight(n((R, N)) * 1 / np.sqrt(R) / fr[:, None], "e2m1")
    return {
        "xt_words": xtp[0],
        "xt_scales": xtp[1],
        "xo_words": xop[0],
        "xo_scales": xop[1],
        "w_words": wp[0],
        "w_scales": wp[1],
        "w2_words": w2p[0],
        "w2_scales": w2p[1],
        "ca": e4m3fn_bytes(60.0 * n((R, V))),
        "st": (np.random.uniform(0.008, 0.024, (R, 1)) * fr[:, None]).astype(np.float32),
        "wb_words": wbp[0],
        "wb_scales": wbp[1],
        "offs": striped(idx),
        "offs2": striped(idx2),
        "offs3": striped(idx3),
        "offs4": striped(idx4),
        "offs5": striped(idx5),
    }


def reference(xt_words, xt_scales, xo_words, xo_scales, w_words, w_scales, w2_words, w2_scales, ca, st, wb_words, wb_scales, offs, offs2, offs3, offs4, offs5):
    idx = unstriped(offs)
    idx2 = unstriped(offs2)
    idx3 = unstriped(offs3)
    idx4 = unstriped(offs4)
    idx5 = unstriped(offs5)
    xtu = unpack_weight(xt_words, xt_scales, "e5m2")
    xou = unpack_weight(xo_words, xo_scales, "e4m3")
    wu = unpack_weight(w_words, w_scales, "e2m1")
    w2u = unpack_weight(w2_words, w2_scales, "e2m1")
    wbu = unpack_weight(wb_words, wb_scales, "e2m1")
    xtidxg = xtu[:, idx]
    a = wu.T @ xtidxg
    xoidx2g = xou[:, idx2]
    b = w2u.T @ xoidx2g
    g1 = e4m3fn_values(ca)[:, idx4] * f64(st)
    hid = np.abs(a[:, idx3] * g1 - b[:, idx5])
    hidq = mxq(hid, 0, "e4m3")
    p = wbu.T @ hidq
    return p

@@ -1,0 +1,185 @@
+from contextlib import ExitStack
+
+import concourse.mybir as mybir
+
+K, T, J, R, V, O, N = 512, 1024, 256, 512, 1024, 128, 256
+P = 128
+PACK = 4
+QUADS = 4
+FLOPS = 2 * K * R * J * 2 + 2 * R * N * O
+
+F32 = mybir.dt.float32
+BF16 = mybir.dt.bfloat16
+I32 = mybir.dt.int32
+U32 = mybir.dt.uint32
+U16 = mybir.dt.uint16
+U8 = mybir.dt.uint8
+E4M3 = mybir.dt.float8_e4m3fn
+E4M3X4 = mybir.dt.float8_e4m3fn_x4
+E5M2X4 = mybir.dt.float8_e5m2_x4
+E2M1X4 = mybir.dt.float4_e2m1fn_x4
+ALU = mybir.AluOpType
+ACT = mybir.ActivationFunctionType
+
+
+def tile_list_reconciled_kernel(tc, xt_words, xt_scales, xo_words, xo_scales, w_words, w_scales,
+                                     w2_words, w2_scales, ca, st, wb_words, wb_scales,
+                                     offs, offs2, offs3, offs4, offs5, out):
+    nc = tc.nc
+    with ExitStack() as ctx:
+        sb = ctx.enter_context(tc.tile_pool(name="sb", bufs=1))
+        ps = ctx.enter_context(tc.psum_pool(name="ps", bufs=1))
+
+        def tile(name, shape, dtype):
+            return sb.tile(shape, dtype, name=name, align_bytes=64)
+
+        def clear(engine, plane):
+            engine.memset(plane[:].bitcast(I32), 0)
+
+        def load_list(name, src):
+            lst = tile(name, list(src.shape), U16)
+            nc.sync.dma_start(lst[:], src)
+            return lst
+
+        def load_scale_rows(queue, plane, scales, quads=range(QUADS)):
+            for q in quads:
+                queue.dma_start(plane[32 * q : 32 * q + 4, :].bitcast(I32), scales[0, 4 * q : 4 * q + 4, :].bitcast(I32))
+
+        def stage_scale_rows(queue, name, scales):
+            width = scales.shape[2]
+            rows = tile(name, [4, QUADS, width // 4], I32)
+            queue.dma_start(rows[:], scales[0].bitcast(I32).rearrange("(q r) n -> r q n", r=4))
+            return rows
+
+        def spread(plane, rows, q):
+            nc.vector.tensor_copy(plane[32 * q : 32 * q + 4, :].bitcast(I32), rows[:, q, :])
+
+        def load_fp8_words(queue, words_tile, words):
+            queue.dma_start(words_tile[:].bitcast(I32), words[0].rearrange("p c r -> p (c r)").bitcast(I32))
+
+        def load_fp4_words(queue, words_tile, words):
+            queue.dma_start(words_tile[:].bitcast(I32), words[0].bitcast(I32))
+
+        def gather(dst, table, lst):
+            nc.vector.tensor_copy(dst, table[:].indirect(lst[:]))
+
+        def deal_words(dst, src):
+            nc.scalar.copy(dst[:].bitcast(U16).rearrange("p (t m) -> p t m", t=PACK),
+                           src[:].bitcast(U16).rearrange("p (m t) -> p t m", t=PACK))
+
+        def deal_scales(engine, dst, src):
+            engine.tensor_copy(dst[:].rearrange("p (t m) -> p t m", t=PACK),
+                               src[:].rearrange("p (m t) -> p t m", t=PACK))
+
+        def product(bank, wts, wts_scale, block, moving, moving_scale):
+            nc.tensor.matmul_mx(bank[:], lhsT=wts[:, 2 * P * block : 2 * P * (block + 1)].bitcast(E2M1X4),
+                                lhsT_scale=wts_scale[:, P * block : P * (block + 1)],
+                                rhs=moving, rhs_scale=moving_scale, start=True, stop=True)
+
+        xt_w = tile("xt_w", [P, T], U32)
+        xt_s = tile("xt_s", [P, T], U8)
+        xo_w = tile("xo_w", [P, T], U32)
+        xo_s = tile("xo_s", [P, T], U8)
+        w_w = tile("w_w", [P, 2 * R], U8)
+        w_s = tile("w_s", [P, R], U8)
+        w2_w = tile("w2_w", [P, 2 * R], U8)
+        w2_s = tile("w2_s", [P, R], U8)
+        wb_w = tile("wb_w", [P, 2 * N], U8)
+        wb_s = tile("wb_s", [P, N], U8)
+        ca_t = [tile("ca%d" % t, [P, V], U8) for t in range(PACK)]
+        st_t = tile("st_t", [P, PACK], F32)
+        ca_rows = ca.rearrange("(p t) v -> t p v", t=PACK)
+        xt_wg = tile("xt_wg", [P, J], U32)
+        xt_sg = tile("xt_sg", [P, J], U8)
+        xo_wg = tile("xo_wg", [P, J], U32)
+        xo_sg = tile("xo_sg", [P, J], U8)
+        w_wd = tile("w_wd", [P, 2 * R], U8)
+        w_sd = tile("w_sd", [P, R], U8)
+        w2_wd = tile("w2_wd", [P, 2 * R], U8)
+        w2_sd = tile("w2_sd", [P, R], U8)
+        codes = tile("codes", [P, PACK, O], U8)
+        a_sb = [tile("a%d" % t, [P, J], F32) for t in range(PACK)]
+        b_sb = [tile("b%d" % t, [P, J], F32) for t in range(PACK)]
+        a_st = tile("a_st", [P, PACK, O], F32)
+        gained = tile("gained", [P, PACK, O], F32)
+        diff = tile("diff", [P, PACK, O], F32)
+        hid = tile("hid", [P, O, PACK], BF16)
+        hid_w = tile("hid_w", [P, O], U32)
+        hid_s = tile("hid_s", [P, O], U8)
+        res = [tile("res%d" % h, [P, O], F32) for h in range(2)]
+
+        clear(nc.vector, xt_s)
+        clear(nc.vector, w_s)
+        clear(nc.vector, xo_s)
+        clear(nc.vector, w2_s)
+        clear(nc.gpsimd, wb_s)
+        l1 = load_list("l1", offs)
+        xt_r = stage_scale_rows(nc.scalar, "xt_r", xt_scales)
+        load_fp8_words(nc.sync, xt_w, xt_words)
+        w_r = stage_scale_rows(nc.scalar, "w_r", w_scales)
+        load_fp4_words(nc.sync, w_w, w_words)
+        xo_r = stage_scale_rows(nc.scalar, "xo_r", xo_scales)
+        w2_r = stage_scale_rows(nc.sync, "w2_r", w2_scales)
+        load_fp8_words(nc.sync, xo_w, xo_words)
+        l2 = load_list("l2", offs2)
+        load_fp4_words(nc.sync, w2_w, w2_words)
+        nc.gpsimd.dma_start(st_t[:], st.rearrange("(p t) o -> p (t o)", t=PACK))
+        l3 = load_list("l3", offs3)
+        l4 = load_list("l4", offs4)
+        for t in range(PACK):
+            nc.sync.dma_start(ca_t[t][:], ca_rows[t])
+        l5 = load_list("l5", offs5)
+        load_fp4_words(nc.sync, wb_w, wb_words)
+        load_scale_rows(nc.sync, wb_s, wb_scales)
+        for q in range(QUADS):
+            spread(xt_s, xt_r, q)
+            spread(w_s, w_r, q)
+        gather(xt_sg[:], xt_s, l1)
+        gather(xt_wg[:], xt_w, l1)
+        deal_words(w_wd, w_w)
+        deal_scales(nc.gpsimd, w_sd, w_s)
+        a_ps = [ps.tile([P, J], F32, name="a_ps%d" % t, tag="bank%d" % t) for t in range(PACK)]
+        b_ps = [ps.tile([P, J], F32, name="b_ps%d" % t, tag="bank%d" % (PACK + t)) for t in range(PACK)]
+        for t in range(PACK):
+            product(a_ps[t], w_wd, w_sd, t, xt_wg[:].bitcast(E5M2X4), xt_sg[:])
+        deal_words(w2_wd, w2_w)
+        for q in range(QUADS):
+            spread(w2_s, w2_r, q)
+            spread(xo_s, xo_r, q)
+        deal_scales(nc.gpsimd, w2_sd, w2_s)
+        gather(xo_wg[:], xo_w, l2)
+        gather(xo_sg[:], xo_s, l2)
+        for t in range(PACK):
+            product(b_ps[t], w2_wd, w2_sd, t, xo_wg[:].bitcast(E4M3X4), xo_sg[:])
+        for t in range(PACK):
+            nc.scalar.copy(a_sb[t][:], a_ps[t][:])
+        for t in range(PACK):
+            nc.scalar.activation(a_st[:, t, :], a_sb[t][:].indirect(l3[:]), ACT.Copy, scale=st_t[:, t : t + 1])
+        b_g = tile("b_g", [P, 2, O], F32)
+
+        def gain(lo):
+            nc.vector.tensor_tensor(gained[:, lo : lo + 2, :].rearrange("p t o -> p (t o)"),
+                                    codes[:, lo : lo + 2, :].rearrange("p t o -> p (t o)").bitcast(E4M3),
+                                    a_st[:, lo : lo + 2, :].rearrange("p t o -> p (t o)"), ALU.mult)
+
+        for t in range(3):
+            gather(codes[:, t, :], ca_t[t], l4)
+        gain(0)
+        gather(codes[:, 3, :], ca_t[3], l4)
+        for t in range(PACK):
+            nc.scalar.copy(b_sb[t][:], b_ps[t][:])
+        for t in (2, 3):
+            nc.scalar.activation(b_g[:, t - 2, :], b_sb[t][:].indirect(l5[:]), ACT.Copy)
+        nc.vector.tensor_tensor(diff[:, 0, :], b_sb[0][:].indirect(l5[:]), gained[:, 0, :], ALU.subtract)
+        gain(2)
+        nc.vector.tensor_tensor(diff[:, 1, :], b_sb[1][:].indirect(l5[:]), gained[:, 1, :], ALU.subtract)
+        nc.vector.tensor_tensor(diff[:, 2:4, :], b_g[:], gained[:, 2:4, :], ALU.subtract)
+        nc.scalar.activation(hid[:], diff[:].rearrange("p t o -> p o t"), ACT.Abs)
+        nc.vector.quantize_mx(hid_w[:].bitcast(E4M3X4), hid_s[:], hid[:].rearrange("p o t -> p (o t)"))
+        o_ps = [ps.tile([P, O], F32, name="o_ps%d" % h, tag="bank%d" % h) for h in range(2)]
+        for h in range(2):
+            product(o_ps[h], wb_w, wb_s, h, hid_w[:].bitcast(E4M3X4), hid_s[:])
+        nc.vector.tensor_copy(res[0][:], o_ps[0][:])
+        nc.sync.dma_start(out[0:P, :], res[0][:])
+        nc.scalar.copy(res[1][:], o_ps[1][:])
+        nc.scalar.dma_start(out[P : 2 * P, :], res[1][:])

@@ -98,8 +98,6 @@ def tile_list_reconciled_kernel(tc, xt_words, xt_scales, xo_words, xo_scales, w_
         w2_wd = tile("w2_wd", [P, 2 * R], U8)
         w2_sd = tile("w2_sd", [P, R], U8)
         codes = tile("codes", [P, PACK, O], U8)
-        a_sb = [tile("a%d" % t, [P, J], F32) for t in range(PACK)]
-        b_sb = [tile("b%d" % t, [P, J], F32) for t in range(PACK)]
         a_st = tile("a_st", [P, PACK, O], F32)
         gained = tile("gained", [P, PACK, O], F32)
         diff = tile("diff", [P, PACK, O], F32)
@@ -108,22 +106,44 @@ def tile_list_reconciled_kernel(tc, xt_words, xt_scales, xo_words, xo_scales, w_
         hid_s = tile("hid_s", [P, O], U8)
         res = [tile("res%d" % h, [P, O], F32) for h in range(2)]
 
+        xo_r = tile("xo_r", [64, 2, T // 4], I32)
+        w2_r = tile("w2_r", [64, 2, R // 4], I32)
+
+        def load_pairs(queue, dst, scales):
+            rows = scales[0].bitcast(I32).rearrange("(h q r) n -> q r h n", h=2, q=2)
+            for q in range(2):
+                queue.dma_start(dst[32 * q : 32 * q + 4], rows[q])
+
+        def as_halves(plane2):
+            return plane2[:].bitcast(I32).rearrange("p (h n) -> p h n", h=2)
+
+        def unfold(plane2):
+            nc.vector.tensor_copy(as_halves(plane2)[64:128, 0, :], as_halves(plane2)[0:64, 1, :])
+
+        def load_quadrant(queue, plane, scales, q):
+            rows = scales[0, 4 * q : 4 * q + 4, :].bitcast(I32)
+            queue.dma_start(plane[32 * q : 32 * q + 32, :].bitcast(I32), rows.unsqueeze(0).to_broadcast([8, 4, rows.shape[1]]))
+        w_s2 = tile("w_s2", [P, 2 * R], U8)
+
+        def deal_block(dst, src, t):
+            nc.scalar.copy(dst[:].bitcast(U16)[:, P * t : P * (t + 1)], src[:].bitcast(U16)[:, t : R : PACK])
+
+        clear(nc.vector, w_s2)
         clear(nc.vector, xt_s)
-        clear(nc.vector, w_s)
-        clear(nc.vector, xo_s)
-        clear(nc.vector, w2_s)
-        clear(nc.gpsimd, wb_s)
-        l1 = load_list("l1", offs)
-        xt_r = stage_scale_rows(nc.scalar, "xt_r", xt_scales)
-        load_fp8_words(nc.sync, xt_w, xt_words)
-        w_r = stage_scale_rows(nc.scalar, "w_r", w_scales)
-        load_fp4_words(nc.sync, w_w, w_words)
-        xo_r = stage_scale_rows(nc.scalar, "xo_r", xo_scales)
-        w2_r = stage_scale_rows(nc.sync, "w2_r", w2_scales)
-        load_fp8_words(nc.sync, xo_w, xo_words)
-        l2 = load_list("l2", offs2)
-        load_fp4_words(nc.sync, w2_w, w2_words)
+        nc.vector.memset(xo_r[:], 0)
+        clear(nc.vector, wb_s)
+        nc.gpsimd.memset(w2_r[:], 0)
+        load_pairs(nc.gpsimd, w2_r, w2_scales)
         nc.gpsimd.dma_start(st_t[:], st.rearrange("(p t) o -> p (t o)", t=PACK))
+        l1 = load_list("l1", offs)
+        load_pairs(nc.sync, as_halves(w_s2), w_scales)
+        load_scale_rows(nc.scalar, xt_s, xt_scales)
+        load_fp8_words(nc.sync, xt_w, xt_words)
+        load_fp4_words(nc.sync, w_w, w_words)
+        load_pairs(nc.sync, xo_r, xo_scales)
+        l2 = load_list("l2", offs2)
+        load_fp8_words(nc.sync, xo_w, xo_words)
+        load_fp4_words(nc.sync, w2_w, w2_words)
         l3 = load_list("l3", offs3)
         l4 = load_list("l4", offs4)
         for t in range(PACK):
@@ -131,30 +151,33 @@ def tile_list_reconciled_kernel(tc, xt_words, xt_scales, xo_words, xo_scales, w_
         l5 = load_list("l5", offs5)
         load_fp4_words(nc.sync, wb_w, wb_words)
         load_scale_rows(nc.sync, wb_s, wb_scales)
-        for q in range(QUADS):
-            spread(xt_s, xt_r, q)
-            spread(w_s, w_r, q)
+        unfold(w_s2)
+        deal_scales(nc.vector, w_sd, w_s2[:, 0:R])
         gather(xt_sg[:], xt_s, l1)
         gather(xt_wg[:], xt_w, l1)
-        deal_words(w_wd, w_w)
-        deal_scales(nc.gpsimd, w_sd, w_s)
         a_ps = [ps.tile([P, J], F32, name="a_ps%d" % t, tag="bank%d" % t) for t in range(PACK)]
         b_ps = [ps.tile([P, J], F32, name="b_ps%d" % t, tag="bank%d" % (PACK + t)) for t in range(PACK)]
         for t in range(PACK):
+            deal_block(w_wd, w_w, t)
+        for t in range(PACK):
             product(a_ps[t], w_wd, w_sd, t, xt_wg[:].bitcast(E5M2X4), xt_sg[:])
-        deal_words(w2_wd, w2_w)
-        for q in range(QUADS):
-            spread(w2_s, w2_r, q)
-            spread(xo_s, xo_r, q)
-        deal_scales(nc.gpsimd, w2_sd, w2_s)
-        gather(xo_wg[:], xo_w, l2)
+        for h in range(2):
+            nc.vector.tensor_copy(xo_s[64 * h : 64 * h + 64, :].bitcast(I32), xo_r[:, h, :])
         gather(xo_sg[:], xo_s, l2)
+        w2_p = sb.tile([P, R], U8, name="w2_p", tag="xo_s", align_bytes=64)
+        for h in range(2):
+            nc.vector.tensor_copy(w2_p[64 * h : 64 * h + 64, :].bitcast(I32), w2_r[:, h, :])
+        deal_scales(nc.vector, w2_sd, w2_p)
+        gather(xo_wg[:], xo_w, l2)
+        a_sb = [sb.tile([P, J], F32, name="a%d" % t, tag="rows%d" % t, align_bytes=64) for t in range(PACK)]
+        for t in range(PACK):
+            nc.scalar.copy(a_sb[t][:], a_ps[t][:])
+        deal_words(w2_wd, w2_w)
         for t in range(PACK):
             product(b_ps[t], w2_wd, w2_sd, t, xo_wg[:].bitcast(E4M3X4), xo_sg[:])
         for t in range(PACK):
-            nc.scalar.copy(a_sb[t][:], a_ps[t][:])
-        for t in range(PACK):
             nc.scalar.activation(a_st[:, t, :], a_sb[t][:].indirect(l3[:]), ACT.Copy, scale=st_t[:, t : t + 1])
+        b_sb = [sb.tile([P, J], F32, name="b%d" % t, tag="rows%d" % t, align_bytes=64) for t in range(PACK)]
         b_g = tile("b_g", [P, 2, O], F32)
 
         def gain(lo):

@@ -134,45 +134,46 @@ def tile_list_reconciled_kernel(tc, xt_words, xt_scales, xo_words, xo_scales, w_
         clear(nc.vector, wb_s)
         nc.gpsimd.memset(w2_r[:], 0)
         load_pairs(nc.gpsimd, w2_r, w2_scales)
-        nc.gpsimd.dma_start(st_t[:], st.rearrange("(p t) o -> p (t o)", t=PACK))
         l1 = load_list("l1", offs)
         load_pairs(nc.sync, as_halves(w_s2), w_scales)
         load_scale_rows(nc.scalar, xt_s, xt_scales)
         load_fp8_words(nc.sync, xt_w, xt_words)
         load_fp4_words(nc.sync, w_w, w_words)
-        load_pairs(nc.sync, xo_r, xo_scales)
-        l2 = load_list("l2", offs2)
-        load_fp8_words(nc.sync, xo_w, xo_words)
         load_fp4_words(nc.sync, w2_w, w2_words)
+        load_pairs(nc.sync, xo_r, xo_scales)
+        load_fp8_words(nc.sync, xo_w, xo_words)
+        l2 = load_list("l2", offs2)
         l3 = load_list("l3", offs3)
+        nc.sync.dma_start(st_t[:], st.rearrange("(p t) o -> p (t o)", t=PACK))
         l4 = load_list("l4", offs4)
-        for t in range(PACK):
+        for t in range(PACK - 1):
             nc.sync.dma_start(ca_t[t][:], ca_rows[t])
         l5 = load_list("l5", offs5)
+        nc.sync.dma_start(ca_t[PACK - 1][:], ca_rows[PACK - 1])
         load_fp4_words(nc.sync, wb_w, wb_words)
         load_scale_rows(nc.sync, wb_s, wb_scales)
         unfold(w_s2)
-        deal_scales(nc.vector, w_sd, w_s2[:, 0:R])
+        deal_scales(nc.gpsimd, w_sd, w_s2[:, 0:R])
         gather(xt_sg[:], xt_s, l1)
         gather(xt_wg[:], xt_w, l1)
         a_ps = [ps.tile([P, J], F32, name="a_ps%d" % t, tag="bank%d" % t) for t in range(PACK)]
         b_ps = [ps.tile([P, J], F32, name="b_ps%d" % t, tag="bank%d" % (PACK + t)) for t in range(PACK)]
         for t in range(PACK):
             deal_block(w_wd, w_w, t)
+        deal_words(w2_wd, w2_w)
         for t in range(PACK):
             product(a_ps[t], w_wd, w_sd, t, xt_wg[:].bitcast(E5M2X4), xt_sg[:])
         for h in range(2):
             nc.vector.tensor_copy(xo_s[64 * h : 64 * h + 64, :].bitcast(I32), xo_r[:, h, :])
-        gather(xo_sg[:], xo_s, l2)
-        w2_p = sb.tile([P, R], U8, name="w2_p", tag="xo_s", align_bytes=64)
+        w2_p = sb.tile([P, R], U8, name="w2_p", tag="xo_r", align_bytes=64)
         for h in range(2):
             nc.vector.tensor_copy(w2_p[64 * h : 64 * h + 64, :].bitcast(I32), w2_r[:, h, :])
-        deal_scales(nc.vector, w2_sd, w2_p)
+        deal_scales(nc.gpsimd, w2_sd, w2_p)
         gather(xo_wg[:], xo_w, l2)
+        gather(xo_sg[:], xo_s, l2)
         a_sb = [sb.tile([P, J], F32, name="a%d" % t, tag="rows%d" % t, align_bytes=64) for t in range(PACK)]
         for t in range(PACK):
             nc.scalar.copy(a_sb[t][:], a_ps[t][:])
-        deal_words(w2_wd, w2_w)
         for t in range(PACK):
             product(b_ps[t], w2_wd, w2_sd, t, xo_wg[:].bitcast(E4M3X4), xo_sg[:])
         for t in range(PACK):
@@ -197,7 +198,8 @@ def tile_list_reconciled_kernel(tc, xt_words, xt_scales, xo_words, xo_scales, w_
         gain(2)
         nc.vector.tensor_tensor(diff[:, 1, :], b_sb[1][:].indirect(l5[:]), gained[:, 1, :], ALU.subtract)
         nc.vector.tensor_tensor(diff[:, 2:4, :], b_g[:], gained[:, 2:4, :], ALU.subtract)
-        nc.scalar.activation(hid[:], diff[:].rearrange("p t o -> p o t"), ACT.Abs)
+        for lo in (0, 2):
+            nc.scalar.activation(hid[:, :, lo : lo + 2], diff[:, lo : lo + 2, :].rearrange("p t o -> p o t"), ACT.Abs)
         nc.vector.quantize_mx(hid_w[:].bitcast(E4M3X4), hid_s[:], hid[:].rearrange("p o t -> p (o t)"))
         o_ps = [ps.tile([P, O], F32, name="o_ps%d" % h, tag="bank%d" % h) for h in range(2)]
         for h in range(2):

@@ -129,14 +129,14 @@ def tile_list_reconciled_kernel(tc, xt_words, xt_scales, xo_words, xo_scales, w_
             nc.scalar.copy(dst[:].bitcast(U16)[:, P * t : P * (t + 1)], src[:].bitcast(U16)[:, t : R : PACK])
 
         clear(nc.vector, w_s2)
-        clear(nc.vector, xt_s)
         nc.vector.memset(xo_r[:], 0)
         clear(nc.vector, wb_s)
         nc.gpsimd.memset(w2_r[:], 0)
         load_pairs(nc.gpsimd, w2_r, w2_scales)
         l1 = load_list("l1", offs)
         load_pairs(nc.sync, as_halves(w_s2), w_scales)
-        load_scale_rows(nc.scalar, xt_s, xt_scales)
+        for q in range(QUADS):
+            load_quadrant(nc.scalar, xt_s, xt_scales, q)
         load_fp8_words(nc.sync, xt_w, xt_words)
         load_fp4_words(nc.sync, w_w, w_words)
         load_fp4_words(nc.sync, w2_w, w2_words)
@@ -146,10 +146,9 @@ def tile_list_reconciled_kernel(tc, xt_words, xt_scales, xo_words, xo_scales, w_
         l3 = load_list("l3", offs3)
         nc.sync.dma_start(st_t[:], st.rearrange("(p t) o -> p (t o)", t=PACK))
         l4 = load_list("l4", offs4)
-        for t in range(PACK - 1):
+        for t in range(PACK):
             nc.sync.dma_start(ca_t[t][:], ca_rows[t])
         l5 = load_list("l5", offs5)
-        nc.sync.dma_start(ca_t[PACK - 1][:], ca_rows[PACK - 1])
         load_fp4_words(nc.sync, wb_w, wb_words)
         load_scale_rows(nc.sync, wb_s, wb_scales)
         unfold(w_s2)
@@ -160,11 +159,12 @@ def tile_list_reconciled_kernel(tc, xt_words, xt_scales, xo_words, xo_scales, w_
         b_ps = [ps.tile([P, J], F32, name="b_ps%d" % t, tag="bank%d" % (PACK + t)) for t in range(PACK)]
         for t in range(PACK):
             deal_block(w_wd, w_w, t)
-        deal_words(w2_wd, w2_w)
         for t in range(PACK):
             product(a_ps[t], w_wd, w_sd, t, xt_wg[:].bitcast(E5M2X4), xt_sg[:])
         for h in range(2):
             nc.vector.tensor_copy(xo_s[64 * h : 64 * h + 64, :].bitcast(I32), xo_r[:, h, :])
+        nc.vector.tensor_copy(w2_wd[:].bitcast(U16).rearrange("p (t m) -> p t m", t=PACK),
+                              w2_w[:].bitcast(U16).rearrange("p (m t) -> p t m", t=PACK))
         w2_p = sb.tile([P, R], U8, name="w2_p", tag="xo_r", align_bytes=64)
         for h in range(2):
             nc.vector.tensor_copy(w2_p[64 * h : 64 * h + 64, :].bitcast(I32), w2_r[:, h, :])

@@ -3,10 +3,14 @@ from contextlib import ExitStack
 import concourse.mybir as mybir
 
 K, T, J, R, V, O, N = 512, 1024, 256, 512, 1024, 128, 256
+FLOPS = 2 * (2 * K * R * J) + 2 * R * N * O
+
 P = 128
-PACK = 4
+SLOTS = 4
 QUADS = 4
-FLOPS = 2 * K * R * J * 2 + 2 * R * N * O
+LIVE = 4
+HALF = P // 2
+FUSED = 2
 
 F32 = mybir.dt.float32
 BF16 = mybir.dt.bfloat16
@@ -30,177 +34,158 @@ def tile_list_reconciled_kernel(tc, xt_words, xt_scales, xo_words, xo_scales, w_
         sb = ctx.enter_context(tc.tile_pool(name="sb", bufs=1))
         ps = ctx.enter_context(tc.psum_pool(name="ps", bufs=1))
 
-        def tile(name, shape, dtype):
-            return sb.tile(shape, dtype, name=name, align_bytes=64)
-
-        def clear(engine, plane):
-            engine.memset(plane[:].bitcast(I32), 0)
+        def tile(name, shape, dtype, tag=None):
+            return sb.tile(shape, dtype, name=name, tag=tag or name, align_bytes=64)
 
         def load_list(name, src):
             lst = tile(name, list(src.shape), U16)
             nc.sync.dma_start(lst[:], src)
             return lst
 
-        def load_scale_rows(queue, plane, scales, quads=range(QUADS)):
-            for q in quads:
-                queue.dma_start(plane[32 * q : 32 * q + 4, :].bitcast(I32), scales[0, 4 * q : 4 * q + 4, :].bitcast(I32))
+        def load_fp8_words(dst, words):
+            nc.sync.dma_start(dst[:].bitcast(I32), words[0].rearrange("p c r -> p (c r)").bitcast(I32))
 
-        def stage_scale_rows(queue, name, scales):
-            width = scales.shape[2]
-            rows = tile(name, [4, QUADS, width // 4], I32)
-            queue.dma_start(rows[:], scales[0].bitcast(I32).rearrange("(q r) n -> r q n", r=4))
-            return rows
+        def load_fp4_words(dst, words):
+            nc.sync.dma_start(dst[:].bitcast(I32), words[0].bitcast(I32))
 
-        def spread(plane, rows, q):
-            nc.vector.tensor_copy(plane[32 * q : 32 * q + 4, :].bitcast(I32), rows[:, q, :])
+        def quadrant_rows(scales, q):
+            return scales[0, LIVE * q : LIVE * (q + 1), :].bitcast(I32)
 
-        def load_fp8_words(queue, words_tile, words):
-            queue.dma_start(words_tile[:].bitcast(I32), words[0].rearrange("p c r -> p (c r)").bitcast(I32))
+        def load_scale_pairs(queue, dst, scales):
+            rows = scales[0].bitcast(I32).rearrange("(h q r) n -> q r h n", h=2, q=2)
+            for q in range(2):
+                queue.dma_start(dst[32 * q : 32 * q + LIVE], rows[q])
 
-        def load_fp4_words(queue, words_tile, words):
-            queue.dma_start(words_tile[:].bitcast(I32), words[0].bitcast(I32))
+        def pairs_to_plane(plane, pairs, h):
+            nc.vector.tensor_copy(plane[HALF * h : HALF * (h + 1), :].bitcast(I32), pairs[0:HALF, h, :])
+
+        def dealt(ap):
+            return ap.rearrange("p (t m) -> p t m", t=SLOTS)
+
+        def undealt(ap):
+            return ap.rearrange("p (m t) -> p t m", t=SLOTS)
 
         def gather(dst, table, lst):
             nc.vector.tensor_copy(dst, table[:].indirect(lst[:]))
 
-        def deal_words(dst, src):
-            nc.scalar.copy(dst[:].bitcast(U16).rearrange("p (t m) -> p t m", t=PACK),
-                           src[:].bitcast(U16).rearrange("p (m t) -> p t m", t=PACK))
+        def product(bank, words, plane, block, moving, moving_plane):
+            nc.tensor.matmul_mx(bank[:], lhsT=words[:, 2 * P * block : 2 * P * (block + 1)].bitcast(E2M1X4),
+                                lhsT_scale=plane[:, P * block : P * (block + 1)],
+                                rhs=moving, rhs_scale=moving_plane, start=True, stop=True)
 
-        def deal_scales(engine, dst, src):
-            engine.tensor_copy(dst[:].rearrange("p (t m) -> p t m", t=PACK),
-                               src[:].rearrange("p (m t) -> p t m", t=PACK))
-
-        def product(bank, wts, wts_scale, block, moving, moving_scale):
-            nc.tensor.matmul_mx(bank[:], lhsT=wts[:, 2 * P * block : 2 * P * (block + 1)].bitcast(E2M1X4),
-                                lhsT_scale=wts_scale[:, P * block : P * (block + 1)],
-                                rhs=moving, rhs_scale=moving_scale, start=True, stop=True)
+        def flat(ap):
+            return ap.rearrange("p t o -> p (t o)")
 
         xt_w = tile("xt_w", [P, T], U32)
         xt_s = tile("xt_s", [P, T], U8)
         xo_w = tile("xo_w", [P, T], U32)
-        xo_s = tile("xo_s", [P, T], U8)
+        xo_pairs = tile("xo_pairs", [HALF, 2, T // 4], I32)
         w_w = tile("w_w", [P, 2 * R], U8)
-        w_s = tile("w_s", [P, R], U8)
+        w_s = tile("w_s", [P, 2 * R], U8)
+        w_pairs = w_s[:].bitcast(I32).rearrange("p (h n) -> p h n", h=2)
         w2_w = tile("w2_w", [P, 2 * R], U8)
-        w2_s = tile("w2_s", [P, R], U8)
+        w2_pairs = tile("w2_pairs", [HALF, 2, R // 4], I32)
         wb_w = tile("wb_w", [P, 2 * N], U8)
         wb_s = tile("wb_s", [P, N], U8)
-        ca_t = [tile("ca%d" % t, [P, V], U8) for t in range(PACK)]
-        st_t = tile("st_t", [P, PACK], F32)
-        ca_rows = ca.rearrange("(p t) v -> t p v", t=PACK)
+        ca_t = [tile("ca%d" % t, [P, V], U8) for t in range(SLOTS)]
+        st_t = tile("st_t", [P, SLOTS], F32)
+
+        nc.vector.memset(w_s[:].bitcast(I32), 0)
+        nc.vector.memset(xo_pairs[:], 0)
+        nc.vector.memset(wb_s[:].bitcast(I32), 0)
+        nc.gpsimd.memset(w2_pairs[:], 0)
+
+        load_scale_pairs(nc.gpsimd, w2_pairs, w2_scales)
+        idx = load_list("idx", offs)
+        load_scale_pairs(nc.sync, w_pairs, w_scales)
+        for q in range(QUADS):
+            nc.scalar.dma_start(xt_s[32 * q : 32 * (q + 1), :].bitcast(I32),
+                                quadrant_rows(xt_scales, q).unsqueeze(0).to_broadcast([32 // LIVE, LIVE, T // 4]))
+        load_fp8_words(xt_w, xt_words)
+        load_fp4_words(w_w, w_words)
+        load_fp4_words(w2_w, w2_words)
+        load_scale_pairs(nc.sync, xo_pairs, xo_scales)
+        idx2 = load_list("idx2", offs2)
+        load_fp8_words(xo_w, xo_words)
+        idx3 = load_list("idx3", offs3)
+        nc.sync.dma_start(st_t[:], st.rearrange("(p t) o -> p (t o)", t=SLOTS))
+        idx4 = load_list("idx4", offs4)
+        ca_rows = ca.rearrange("(p t) v -> t p v", t=SLOTS)
+        for t in range(SLOTS):
+            nc.sync.dma_start(ca_t[t][:], ca_rows[t])
+        idx5 = load_list("idx5", offs5)
+        load_fp4_words(wb_w, wb_words)
+        for q in range(QUADS):
+            nc.sync.dma_start(wb_s[32 * q : 32 * q + LIVE, :].bitcast(I32), quadrant_rows(wb_scales, q))
+
+        w_sd = tile("w_sd", [P, R], U8)
+        w_wd = tile("w_wd", [P, 2 * R], U8)
+        w2_wd = tile("w2_wd", [P, 2 * R], U8)
         xt_wg = tile("xt_wg", [P, J], U32)
         xt_sg = tile("xt_sg", [P, J], U8)
+        nc.vector.tensor_copy(w_pairs[HALF:P, 0, :], w_pairs[0:HALF, 1, :])
+        nc.gpsimd.tensor_copy(dealt(w_sd[:]), undealt(w_s[:, 0:R]))
+        gather(xt_sg[:], xt_s, idx)
+        gather(xt_wg[:], xt_w, idx)
+        for t in range(SLOTS):
+            nc.scalar.copy(dealt(w_wd[:].bitcast(U16))[:, t, :], undealt(w_w[:].bitcast(U16))[:, t, :])
+        nc.scalar.copy(dealt(w2_wd[:].bitcast(U16)), undealt(w2_w[:].bitcast(U16)))
+        a_ps = [ps.tile([P, J], F32, name="a_ps%d" % t, tag="bank%d" % t) for t in range(SLOTS)]
+        b_ps = [ps.tile([P, J], F32, name="b_ps%d" % t, tag="bank%d" % (SLOTS + t)) for t in range(SLOTS)]
+        for t in range(SLOTS):
+            product(a_ps[t], w_wd, w_sd, t, xt_wg[:].bitcast(E5M2X4), xt_sg[:])
+
+        xo_s = tile("xo_s", [P, T], U8)
+        w2_sd = tile("w2_sd", [P, R], U8)
         xo_wg = tile("xo_wg", [P, J], U32)
         xo_sg = tile("xo_sg", [P, J], U8)
-        w_wd = tile("w_wd", [P, 2 * R], U8)
-        w_sd = tile("w_sd", [P, R], U8)
-        w2_wd = tile("w2_wd", [P, 2 * R], U8)
-        w2_sd = tile("w2_sd", [P, R], U8)
-        codes = tile("codes", [P, PACK, O], U8)
-        a_st = tile("a_st", [P, PACK, O], F32)
-        gained = tile("gained", [P, PACK, O], F32)
-        diff = tile("diff", [P, PACK, O], F32)
-        hid = tile("hid", [P, O, PACK], BF16)
-        hid_w = tile("hid_w", [P, O], U32)
-        hid_s = tile("hid_s", [P, O], U8)
-        res = [tile("res%d" % h, [P, O], F32) for h in range(2)]
-
-        xo_r = tile("xo_r", [64, 2, T // 4], I32)
-        w2_r = tile("w2_r", [64, 2, R // 4], I32)
-
-        def load_pairs(queue, dst, scales):
-            rows = scales[0].bitcast(I32).rearrange("(h q r) n -> q r h n", h=2, q=2)
-            for q in range(2):
-                queue.dma_start(dst[32 * q : 32 * q + 4], rows[q])
-
-        def as_halves(plane2):
-            return plane2[:].bitcast(I32).rearrange("p (h n) -> p h n", h=2)
-
-        def unfold(plane2):
-            nc.vector.tensor_copy(as_halves(plane2)[64:128, 0, :], as_halves(plane2)[0:64, 1, :])
-
-        def load_quadrant(queue, plane, scales, q):
-            rows = scales[0, 4 * q : 4 * q + 4, :].bitcast(I32)
-            queue.dma_start(plane[32 * q : 32 * q + 32, :].bitcast(I32), rows.unsqueeze(0).to_broadcast([8, 4, rows.shape[1]]))
-        w_s2 = tile("w_s2", [P, 2 * R], U8)
-
-        def deal_block(dst, src, t):
-            nc.scalar.copy(dst[:].bitcast(U16)[:, P * t : P * (t + 1)], src[:].bitcast(U16)[:, t : R : PACK])
-
-        clear(nc.vector, w_s2)
-        nc.vector.memset(xo_r[:], 0)
-        clear(nc.vector, wb_s)
-        nc.gpsimd.memset(w2_r[:], 0)
-        load_pairs(nc.gpsimd, w2_r, w2_scales)
-        l1 = load_list("l1", offs)
-        load_pairs(nc.sync, as_halves(w_s2), w_scales)
-        for q in range(QUADS):
-            load_quadrant(nc.scalar, xt_s, xt_scales, q)
-        load_fp8_words(nc.sync, xt_w, xt_words)
-        load_fp4_words(nc.sync, w_w, w_words)
-        load_fp4_words(nc.sync, w2_w, w2_words)
-        load_pairs(nc.sync, xo_r, xo_scales)
-        load_fp8_words(nc.sync, xo_w, xo_words)
-        l2 = load_list("l2", offs2)
-        l3 = load_list("l3", offs3)
-        nc.sync.dma_start(st_t[:], st.rearrange("(p t) o -> p (t o)", t=PACK))
-        l4 = load_list("l4", offs4)
-        for t in range(PACK):
-            nc.sync.dma_start(ca_t[t][:], ca_rows[t])
-        l5 = load_list("l5", offs5)
-        load_fp4_words(nc.sync, wb_w, wb_words)
-        load_scale_rows(nc.sync, wb_s, wb_scales)
-        unfold(w_s2)
-        deal_scales(nc.gpsimd, w_sd, w_s2[:, 0:R])
-        gather(xt_sg[:], xt_s, l1)
-        gather(xt_wg[:], xt_w, l1)
-        a_ps = [ps.tile([P, J], F32, name="a_ps%d" % t, tag="bank%d" % t) for t in range(PACK)]
-        b_ps = [ps.tile([P, J], F32, name="b_ps%d" % t, tag="bank%d" % (PACK + t)) for t in range(PACK)]
-        for t in range(PACK):
-            deal_block(w_wd, w_w, t)
-        for t in range(PACK):
-            product(a_ps[t], w_wd, w_sd, t, xt_wg[:].bitcast(E5M2X4), xt_sg[:])
         for h in range(2):
-            nc.vector.tensor_copy(xo_s[64 * h : 64 * h + 64, :].bitcast(I32), xo_r[:, h, :])
-        nc.vector.tensor_copy(w2_wd[:].bitcast(U16).rearrange("p (t m) -> p t m", t=PACK),
-                              w2_w[:].bitcast(U16).rearrange("p (m t) -> p t m", t=PACK))
-        w2_p = sb.tile([P, R], U8, name="w2_p", tag="xo_r", align_bytes=64)
-        for h in range(2):
-            nc.vector.tensor_copy(w2_p[64 * h : 64 * h + 64, :].bitcast(I32), w2_r[:, h, :])
-        deal_scales(nc.gpsimd, w2_sd, w2_p)
-        gather(xo_wg[:], xo_w, l2)
-        gather(xo_sg[:], xo_s, l2)
-        a_sb = [sb.tile([P, J], F32, name="a%d" % t, tag="rows%d" % t, align_bytes=64) for t in range(PACK)]
-        for t in range(PACK):
+            pairs_to_plane(xo_s, xo_pairs, h)
+        w2_s = tile("w2_s", [P, R], U8, tag="xo_pairs")
+        for h in reversed(range(2)):
+            pairs_to_plane(w2_s, w2_pairs, h)
+        nc.gpsimd.tensor_copy(dealt(w2_sd[:]), undealt(w2_s[:]))
+        gather(xo_sg[:], xo_s, idx2)
+        gather(xo_wg[:], xo_w, idx2)
+        a_sb = [tile("a%d" % t, [P, J], F32, tag="rows%d" % t) for t in range(SLOTS)]
+        for t in range(SLOTS):
             nc.scalar.copy(a_sb[t][:], a_ps[t][:])
-        for t in range(PACK):
+        for t in range(SLOTS):
             product(b_ps[t], w2_wd, w2_sd, t, xo_wg[:].bitcast(E4M3X4), xo_sg[:])
-        for t in range(PACK):
-            nc.scalar.activation(a_st[:, t, :], a_sb[t][:].indirect(l3[:]), ACT.Copy, scale=st_t[:, t : t + 1])
-        b_sb = [sb.tile([P, J], F32, name="b%d" % t, tag="rows%d" % t, align_bytes=64) for t in range(PACK)]
-        b_g = tile("b_g", [P, 2, O], F32)
+
+        a_st = tile("a_st", [P, SLOTS, O], F32)
+        codes = tile("codes", [P, SLOTS, O], U8)
+        gained = tile("gained", [P, SLOTS, O], F32)
+        b_g = tile("b_g", [P, SLOTS - FUSED, O], F32)
+        diff = tile("diff", [P, SLOTS, O], F32)
 
         def gain(lo):
-            nc.vector.tensor_tensor(gained[:, lo : lo + 2, :].rearrange("p t o -> p (t o)"),
-                                    codes[:, lo : lo + 2, :].rearrange("p t o -> p (t o)").bitcast(E4M3),
-                                    a_st[:, lo : lo + 2, :].rearrange("p t o -> p (t o)"), ALU.mult)
+            pair = slice(lo, lo + 2)
+            nc.vector.tensor_tensor(flat(gained[:, pair, :]), flat(codes[:, pair, :]).bitcast(E4M3),
+                                    flat(a_st[:, pair, :]), ALU.mult)
 
-        for t in range(3):
-            gather(codes[:, t, :], ca_t[t], l4)
-        gain(0)
-        gather(codes[:, 3, :], ca_t[3], l4)
-        for t in range(PACK):
+        for t in range(SLOTS):
+            nc.scalar.activation(a_st[:, t, :], a_sb[t][:].indirect(idx3[:]), ACT.Copy, scale=st_t[:, t : t + 1])
+        b_sb = [tile("b%d" % t, [P, J], F32, tag="rows%d" % t) for t in range(SLOTS)]
+        for t in range(SLOTS):
+            gather(codes[:, t, :], ca_t[t], idx4)
+        for t in range(SLOTS):
             nc.scalar.copy(b_sb[t][:], b_ps[t][:])
-        for t in (2, 3):
-            nc.scalar.activation(b_g[:, t - 2, :], b_sb[t][:].indirect(l5[:]), ACT.Copy)
-        nc.vector.tensor_tensor(diff[:, 0, :], b_sb[0][:].indirect(l5[:]), gained[:, 0, :], ALU.subtract)
+        for t in range(FUSED, SLOTS):
+            nc.scalar.activation(b_g[:, t - FUSED, :], b_sb[t][:].indirect(idx5[:]), ACT.Copy)
+        gain(0)
         gain(2)
-        nc.vector.tensor_tensor(diff[:, 1, :], b_sb[1][:].indirect(l5[:]), gained[:, 1, :], ALU.subtract)
-        nc.vector.tensor_tensor(diff[:, 2:4, :], b_g[:], gained[:, 2:4, :], ALU.subtract)
+        for t in range(FUSED):
+            nc.vector.tensor_tensor(diff[:, t, :], b_sb[t][:].indirect(idx5[:]), gained[:, t, :], ALU.subtract)
+        nc.vector.tensor_tensor(diff[:, FUSED:, :], b_g[:], gained[:, FUSED:, :], ALU.subtract)
+
+        hid = tile("hid", [P, O, SLOTS], BF16)
+        hid_w = tile("hid_w", [P, O], U32)
+        hid_s = tile("hid_s", [P, O], U8)
         for lo in (0, 2):
             nc.scalar.activation(hid[:, :, lo : lo + 2], diff[:, lo : lo + 2, :].rearrange("p t o -> p o t"), ACT.Abs)
         nc.vector.quantize_mx(hid_w[:].bitcast(E4M3X4), hid_s[:], hid[:].rearrange("p o t -> p (o t)"))
+        res = [tile("res%d" % h, [P, O], F32) for h in range(2)]
         o_ps = [ps.tile([P, O], F32, name="o_ps%d" % h, tag="bank%d" % h) for h in range(2)]
         for h in range(2):
             product(o_ps[h], wb_w, wb_s, h, hid_w[:].bitcast(E4M3X4), hid_s[:])

from contextlib import ExitStack

import concourse.mybir as mybir

K, T, J, R, V, O, N = 512, 1024, 256, 512, 1024, 128, 256
FLOPS = 2 * (2 * K * R * J) + 2 * R * N * O

P = 128
SLOTS = 4
QUADS = 4
LIVE = 4
HALF = P // 2
FUSED = 2

F32 = mybir.dt.float32
BF16 = mybir.dt.bfloat16
I32 = mybir.dt.int32
U32 = mybir.dt.uint32
U16 = mybir.dt.uint16
U8 = mybir.dt.uint8
E4M3 = mybir.dt.float8_e4m3fn
E4M3X4 = mybir.dt.float8_e4m3fn_x4
E5M2X4 = mybir.dt.float8_e5m2_x4
E2M1X4 = mybir.dt.float4_e2m1fn_x4
ALU = mybir.AluOpType
ACT = mybir.ActivationFunctionType


def tile_list_reconciled_kernel(tc, xt_words, xt_scales, xo_words, xo_scales, w_words, w_scales,
                                     w2_words, w2_scales, ca, st, wb_words, wb_scales,
                                     offs, offs2, offs3, offs4, offs5, out):
    nc = tc.nc
    with ExitStack() as ctx:
        sb = ctx.enter_context(tc.tile_pool(name="sb", bufs=1))
        ps = ctx.enter_context(tc.psum_pool(name="ps", bufs=1))

        def tile(name, shape, dtype, tag=None):
            return sb.tile(shape, dtype, name=name, tag=tag or name, align_bytes=64)

        def load_list(name, src):
            lst = tile(name, list(src.shape), U16)
            nc.sync.dma_start(lst[:], src)
            return lst

        def load_fp8_words(dst, words):
            nc.sync.dma_start(dst[:].bitcast(I32), words[0].rearrange("p c r -> p (c r)").bitcast(I32))

        def load_fp4_words(dst, words):
            nc.sync.dma_start(dst[:].bitcast(I32), words[0].bitcast(I32))

        def quadrant_rows(scales, q):
            return scales[0, LIVE * q : LIVE * (q + 1), :].bitcast(I32)

        def load_scale_pairs(queue, dst, scales):
            rows = scales[0].bitcast(I32).rearrange("(h q r) n -> q r h n", h=2, q=2)
            for q in range(2):
                queue.dma_start(dst[32 * q : 32 * q + LIVE], rows[q])

        def pairs_to_plane(plane, pairs, h):
            nc.vector.tensor_copy(plane[HALF * h : HALF * (h + 1), :].bitcast(I32), pairs[0:HALF, h, :])

        def dealt(ap):
            return ap.rearrange("p (t m) -> p t m", t=SLOTS)

        def undealt(ap):
            return ap.rearrange("p (m t) -> p t m", t=SLOTS)

        def gather(dst, table, lst):
            nc.vector.tensor_copy(dst, table[:].indirect(lst[:]))

        def product(bank, words, plane, block, moving, moving_plane):
            nc.tensor.matmul_mx(bank[:], lhsT=words[:, 2 * P * block : 2 * P * (block + 1)].bitcast(E2M1X4),
                                lhsT_scale=plane[:, P * block : P * (block + 1)],
                                rhs=moving, rhs_scale=moving_plane, start=True, stop=True)

        def flat(ap):
            return ap.rearrange("p t o -> p (t o)")

        xt_w = tile("xt_w", [P, T], U32)
        xt_s = tile("xt_s", [P, T], U8)
        xo_w = tile("xo_w", [P, T], U32)
        xo_pairs = tile("xo_pairs", [HALF, 2, T // 4], I32)
        w_w = tile("w_w", [P, 2 * R], U8)
        w_s = tile("w_s", [P, 2 * R], U8)
        w_pairs = w_s[:].bitcast(I32).rearrange("p (h n) -> p h n", h=2)
        w2_w = tile("w2_w", [P, 2 * R], U8)
        w2_pairs = tile("w2_pairs", [HALF, 2, R // 4], I32)
        wb_w = tile("wb_w", [P, 2 * N], U8)
        wb_s = tile("wb_s", [P, N], U8)
        ca_t = [tile("ca%d" % t, [P, V], U8) for t in range(SLOTS)]
        st_t = tile("st_t", [P, SLOTS], F32)

        nc.vector.memset(w_s[:].bitcast(I32), 0)
        nc.vector.memset(xo_pairs[:], 0)
        nc.vector.memset(wb_s[:].bitcast(I32), 0)
        nc.gpsimd.memset(w2_pairs[:], 0)

        load_scale_pairs(nc.gpsimd, w2_pairs, w2_scales)
        idx = load_list("idx", offs)
        load_scale_pairs(nc.sync, w_pairs, w_scales)
        for q in range(QUADS):
            nc.scalar.dma_start(xt_s[32 * q : 32 * (q + 1), :].bitcast(I32),
                                quadrant_rows(xt_scales, q).unsqueeze(0).to_broadcast([32 // LIVE, LIVE, T // 4]))
        load_fp8_words(xt_w, xt_words)
        load_fp4_words(w_w, w_words)
        load_fp4_words(w2_w, w2_words)
        load_scale_pairs(nc.sync, xo_pairs, xo_scales)
        idx2 = load_list("idx2", offs2)
        load_fp8_words(xo_w, xo_words)
        idx3 = load_list("idx3", offs3)
        nc.sync.dma_start(st_t[:], st.rearrange("(p t) o -> p (t o)", t=SLOTS))
        idx4 = load_list("idx4", offs4)
        ca_rows = ca.rearrange("(p t) v -> t p v", t=SLOTS)
        for t in range(SLOTS):
            nc.sync.dma_start(ca_t[t][:], ca_rows[t])
        idx5 = load_list("idx5", offs5)
        load_fp4_words(wb_w, wb_words)
        for q in range(QUADS):
            nc.sync.dma_start(wb_s[32 * q : 32 * q + LIVE, :].bitcast(I32), quadrant_rows(wb_scales, q))

        w_sd = tile("w_sd", [P, R], U8)
        w_wd = tile("w_wd", [P, 2 * R], U8)
        w2_wd = tile("w2_wd", [P, 2 * R], U8)
        xt_wg = tile("xt_wg", [P, J], U32)
        xt_sg = tile("xt_sg", [P, J], U8)
        nc.vector.tensor_copy(w_pairs[HALF:P, 0, :], w_pairs[0:HALF, 1, :])
        nc.gpsimd.tensor_copy(dealt(w_sd[:]), undealt(w_s[:, 0:R]))
        gather(xt_sg[:], xt_s, idx)
        gather(xt_wg[:], xt_w, idx)
        for t in range(SLOTS):
            nc.scalar.copy(dealt(w_wd[:].bitcast(U16))[:, t, :], undealt(w_w[:].bitcast(U16))[:, t, :])
        nc.scalar.copy(dealt(w2_wd[:].bitcast(U16)), undealt(w2_w[:].bitcast(U16)))
        a_ps = [ps.tile([P, J], F32, name="a_ps%d" % t, tag="bank%d" % t) for t in range(SLOTS)]
        b_ps = [ps.tile([P, J], F32, name="b_ps%d" % t, tag="bank%d" % (SLOTS + t)) for t in range(SLOTS)]
        for t in range(SLOTS):
            product(a_ps[t], w_wd, w_sd, t, xt_wg[:].bitcast(E5M2X4), xt_sg[:])

        xo_s = tile("xo_s", [P, T], U8)
        w2_sd = tile("w2_sd", [P, R], U8)
        xo_wg = tile("xo_wg", [P, J], U32)
        xo_sg = tile("xo_sg", [P, J], U8)
        for h in range(2):
            pairs_to_plane(xo_s, xo_pairs, h)
        w2_s = tile("w2_s", [P, R], U8, tag="xo_pairs")
        for h in reversed(range(2)):
            pairs_to_plane(w2_s, w2_pairs, h)
        nc.gpsimd.tensor_copy(dealt(w2_sd[:]), undealt(w2_s[:]))
        gather(xo_sg[:], xo_s, idx2)
        gather(xo_wg[:], xo_w, idx2)
        a_sb = [tile("a%d" % t, [P, J], F32, tag="rows%d" % t) for t in range(SLOTS)]
        for t in range(SLOTS):
            nc.scalar.copy(a_sb[t][:], a_ps[t][:])
        for t in range(SLOTS):
            product(b_ps[t], w2_wd, w2_sd, t, xo_wg[:].bitcast(E4M3X4), xo_sg[:])

        a_st = tile("a_st", [P, SLOTS, O], F32)
        codes = tile("codes", [P, SLOTS, O], U8)
        gained = tile("gained", [P, SLOTS, O], F32)
        b_g = tile("b_g", [P, SLOTS - FUSED, O], F32)
        diff = tile("diff", [P, SLOTS, O], F32)

        def gain(lo):
            pair = slice(lo, lo + 2)
            nc.vector.tensor_tensor(flat(gained[:, pair, :]), flat(codes[:, pair, :]).bitcast(E4M3),
                                    flat(a_st[:, pair, :]), ALU.mult)

        for t in range(SLOTS):
            nc.scalar.activation(a_st[:, t, :], a_sb[t][:].indirect(idx3[:]), ACT.Copy, scale=st_t[:, t : t + 1])
        b_sb = [tile("b%d" % t, [P, J], F32, tag="rows%d" % t) for t in range(SLOTS)]
        for t in range(SLOTS):
            gather(codes[:, t, :], ca_t[t], idx4)
        for t in range(SLOTS):
            nc.scalar.copy(b_sb[t][:], b_ps[t][:])
        for t in range(FUSED, SLOTS):
            nc.scalar.activation(b_g[:, t - FUSED, :], b_sb[t][:].indirect(idx5[:]), ACT.Copy)
        gain(0)
        gain(2)
        for t in range(FUSED):
            nc.vector.tensor_tensor(diff[:, t, :], b_sb[t][:].indirect(idx5[:]), gained[:, t, :], ALU.subtract)
        nc.vector.tensor_tensor(diff[:, FUSED:, :], b_g[:], gained[:, FUSED:, :], ALU.subtract)

        hid = tile("hid", [P, O, SLOTS], BF16)
        hid_w = tile("hid_w", [P, O], U32)
        hid_s = tile("hid_s", [P, O], U8)
        for lo in (0, 2):
            nc.scalar.activation(hid[:, :, lo : lo + 2], diff[:, lo : lo + 2, :].rearrange("p t o -> p o t"), ACT.Abs)
        nc.vector.quantize_mx(hid_w[:].bitcast(E4M3X4), hid_s[:], hid[:].rearrange("p o t -> p (o t)"))
        res = [tile("res%d" % h, [P, O], F32) for h in range(2)]
        o_ps = [ps.tile([P, O], F32, name="o_ps%d" % h, tag="bank%d" % h) for h in range(2)]
        for h in range(2):
            product(o_ps[h], wb_w, wb_s, h, hid_w[:].bitcast(E4M3X4), hid_s[:])
        nc.vector.tensor_copy(res[0][:], o_ps[0][:])
        nc.sync.dma_start(out[0:P, :], res[0][:])
        nc.scalar.copy(res[1][:], o_ps[1][:])
        nc.scalar.dma_start(out[P : 2 * P, :], res[1][:])
